import numpy as np
import ml_dtypes


def mxq(x, axis, fmt="e4m3"):
    dtype, down = {"e4m3": (ml_dtypes.float8_e4m3fn, 7), "e5m2": (ml_dtypes.float8_e5m2, 14)}[fmt]
    v = np.moveaxis(np.asarray(x, np.float32).astype(ml_dtypes.bfloat16).astype(np.float64), axis, -1)
    blocks = v.reshape(v.shape[:-1] + (-1, 32))
    amax = np.abs(blocks).max(-1, keepdims=True)
    byte = np.maximum(np.where(amax > 0, np.frexp(amax)[1] - 1 + 127, 0) - down, 1)
    scale = np.exp2(byte - 127.0)
    codes = (blocks / scale).astype(np.float32).astype(dtype).astype(np.float64)
    return np.moveaxis((codes * scale).reshape(v.shape), -1, axis)


WIDE = False


def mx_kscale(k):
    if not WIDE:
        return np.ones(k)
    levels = np.array([10, -10, 5, -5, 0])
    if k % 512:
        return np.exp2(np.random.permutation(np.resize(levels, k // 32))).repeat(32)
    a = np.empty((k // 512, 16))
    for p in range(k // 512):
        a[p, :8] = np.random.permutation(np.resize(levels, 8))
        for g in range(8):
            far = levels[np.abs(levels - a[p, g]) >= 10]
            a[p, g + 8] = far[np.random.randint(len(far))]
    return np.exp2(a.ravel()).repeat(32)


def f64(x):
    return np.asarray(x).astype(np.float64)


def striped8(idx):
    return np.asarray(idx).reshape(8, -1, 16).transpose(0, 2, 1).reshape(128, -1).astype(np.uint16)


def unstriped8(offs):
    return offs.reshape(8, 16, -1).transpose(0, 2, 1).reshape(8, -1).astype(np.int64)


def pick8(x, idx, run):
    r = np.arange(len(x))
    return x[r[:, None], idx[r % (8 * run) // run]]


E2M1 = np.array([0.0, 0.5, 1.0, 1.5, 2.0, 3.0, 4.0, 6.0, -0.0, -0.5, -1.0, -1.5, -2.0, -3.0, -4.0, -6.0])


def pack_weight(w, fmt):
    k, n = w.shape
    w = f64(np.asarray(w, np.float32).astype(ml_dtypes.bfloat16)).reshape(k // 32, 32, n)
    amax = np.abs(w).max(1)
    if fmt == "e4m3":
        byte = np.frexp(amax)[1] - 1 + 127 - 7
    else:
        mant, ex = np.frexp(amax / 6.0)
        byte = np.where(mant > 0.5, ex, ex - 1) + 127
    byte = np.clip(np.where(amax > 0, byte, 1), 1, 254)
    scaled = (w * np.exp2(127.0 - byte)[:, None, :]).reshape(k, n).astype(np.float32)
    by_word = np.ascontiguousarray(scaled.reshape(k // 512, 128, 4, n).transpose(0, 1, 3, 2))
    if fmt == "e4m3":
        words = by_word.astype(ml_dtypes.float8_e4m3fn).view(np.uint8)
    else:
        c = by_word.astype(ml_dtypes.float4_e2m1fn).view(np.uint8) & 0xF
        words = (c[..., 0::2] | (c[..., 1::2] << 4)).reshape(k // 512, 128, 2 * n)
    return np.ascontiguousarray(words), np.ascontiguousarray(byte.astype(np.uint8).reshape(k // 512, 16, n))


def unpack_weight(words, scales, fmt):
    g, _, n = scales.shape
    words = np.ascontiguousarray(words).reshape(g, 128, n, -1)
    if fmt == "e4m3":
        vals = words.view(ml_dtypes.float8_e4m3fn).astype(np.float64)
    else:
        nib = np.empty((g, 128, n, 4), np.uint8)
        nib[..., 0::2] = words & 0xF
        nib[..., 1::2] = words >> 4
        vals = E2M1[nib]
    vals = vals * np.repeat(np.exp2(scales.astype(np.float64) - 127.0), 8, axis=1)[..., None]
    return vals.transpose(0, 1, 3, 2).reshape(g * 512, n)


D, T, Z, I, Q = 512, 1024, 1024, 512, 128


def setup_inputs():
    n = np.random.standard_normal
    idx = np.stack([np.random.permutation(T)[:I] for _ in range(8)])
    idx2 = np.stack([np.random.permutation(T)[:I] for _ in range(8)])
    idx3 = np.stack([np.random.permutation(Z)[:I] for _ in range(8)])
    idx4 = np.stack([np.random.permutation(Z)[:I] for _ in range(8)])
    fd = mx_kscale(D)
    keysp = pack_weight(n((D, T)) / fd[:, None], "e4m3")
    tagsp = pack_weight(n((D, T)) / fd[:, None], "e2m1")
    return {
        "query": (n((D, Q)) * 0.75 / np.sqrt(D) * fd[:, None]).astype(np.float32),
        "query2": (n((D, Q)) * 0.75 / np.sqrt(D) * fd[:, None]).astype(np.float32),
        "keys_words": keysp[0],
        "keys_scales": keysp[1],
        "tags_words": tagsp[0],
        "tags_scales": tagsp[1],
        "old": (1.0 * n((Q, Z))).astype(np.float32),
        "offs": striped8(idx),
        "offs2": striped8(idx2),
        "offs3": striped8(idx3),
        "offs4": striped8(idx4),
    }


def reference(query, query2, keys_words, keys_scales, tags_words, tags_scales, old, offs, offs2, offs3, offs4):
    idx = unstriped8(offs)
    idx2 = unstriped8(offs2)
    idx3 = unstriped8(offs3)
    idx4 = unstriped8(offs4)
    keysu = unpack_weight(keys_words, keys_scales, "e4m3")
    tagsu = unpack_weight(tags_words, tags_scales, "e2m1")
    queryq = mxq(f64(query), 0, "e4m3")
    query2q = mxq(f64(query2), 0, "e4m3")
    a = queryq.T @ keysu + query2q.T @ tagsu
    ta = np.max(a, axis=1, keepdims=True)
    e1 = np.exp(pick8(a, idx, 16) - ta)
    e2 = np.exp(pick8(a, idx2, 16) - ta)
    r = e1 - e2
    f1 = np.zeros((Q, Z))
    f1[np.arange(Q)[:, None], idx3[np.arange(Q) % 128 // 16]] = r
    cc = f64(old) + f1 * 8.0
    y = pick8(cc, idx4, 16)
    return y

@@ -1,0 +1,155 @@
+from contextlib import ExitStack
+
+import concourse.mybir as mybir
+
+D, T, Z, I, Q = 512, 1024, 1024, 512, 128
+FLOPS = 2 * 2 * D * Q * T
+
+F32 = mybir.dt.float32
+BF16 = mybir.dt.bfloat16
+I32 = mybir.dt.int32
+U32 = mybir.dt.uint32
+U16 = mybir.dt.uint16
+U8 = mybir.dt.uint8
+FP8X4 = mybir.dt.float8_e4m3fn_x4
+FP4X4 = mybir.dt.float4_e2m1fn_x4
+ALU = mybir.AluOpType
+ACT = mybir.ActivationFunctionType
+
+P = 128
+PACK = 4
+CHUNK = 256
+HALF = I // 2
+PER_COL = 16
+
+
+def load_scales(nc, plane, scales):
+    for quad in range(4):
+        nc.sync.dma_start(
+            out=plane[32 * quad : 32 * quad + 4, :].bitcast(I32),
+            in_=scales[0, 4 * quad : 4 * quad + 4, :].bitcast(I32),
+        )
+
+
+def quantize_query(nc, pool, raw, name, split):
+    grouped = pool.tile([P, Q, PACK], BF16, name=name + "_grouped", align_bytes=64)
+    codes = pool.tile([P, Q], U32, name=name + "_codes", align_bytes=64)
+    scales = pool.tile([P, Q], U8, name=name + "_scales", align_bytes=64)
+    nc.vector.tensor_copy(
+        out=grouped[:, 0:split, :].rearrange("p (c i) t -> p c t i", i=4),
+        in_=raw[:, :, 0:split].rearrange("p t (c i) -> p c t i", i=4),
+    )
+    if split < Q:
+        nc.scalar.activation(
+            out=grouped[:, split:Q, :].rearrange("p (c i) t -> p c t i", i=4),
+            in_=raw[:, :, split:Q].rearrange("p t (c i) -> p c t i", i=4),
+            func=ACT.Copy,
+        )
+    nc.vector.quantize_mx(
+        out=codes[:].bitcast(FP8X4),
+        scales=scales[:],
+        in_=grouped[:].rearrange("p w t -> p (w t)"),
+    )
+    return codes, scales
+
+
+def tile_attend_passedover_parts_kernel(
+    tc, query, query2, keys_words, keys_scales, tags_words, tags_scales, old, offs, offs2, offs3, offs4, out
+):
+    nc = tc.nc
+    with ExitStack() as ctx:
+        lists = ctx.enter_context(tc.tile_pool(name="lists", bufs=1))
+        sb = ctx.enter_context(tc.tile_pool(name="sb", bufs=1))
+        psum = ctx.enter_context(tc.psum_pool(name="psum", bufs=1))
+
+        tags_plane = sb.tile([P, T], U8, name="tags_plane", align_bytes=64)
+        keys_plane = sb.tile([P, T], U8, name="keys_plane", align_bytes=64)
+        f1 = sb.tile([P, Z], F32, name="f1")
+        nc.vector.memset(tags_plane[:].bitcast(I32), 0)
+        nc.vector.memset(keys_plane[:].bitcast(I32), 0)
+        nc.vector.memset(f1[:], 0.0)
+
+        raw = sb.tile([P, 2, PACK, Q], F32, name="raw", tag="raw_then_old")
+        tags = sb.tile([P, 2 * T], U8, name="tags", align_bytes=64)
+        keys = sb.tile([P, T], U32, name="keys", align_bytes=64)
+        nc.sync.dma_start(out=raw[:, 1], in_=query2.rearrange("(p t) q -> p t q", t=PACK))
+        nc.sync.dma_start(out=tags[:].bitcast(I32), in_=tags_words[0].bitcast(I32))
+        load_scales(nc, tags_plane, tags_scales)
+        nc.sync.dma_start(out=raw[:, 0], in_=query.rearrange("(p t) q -> p t q", t=PACK))
+        nc.sync.dma_start(
+            out=keys[:].bitcast(I32), in_=keys_words[0].rearrange("p n t -> p (n t)").bitcast(I32)
+        )
+        load_scales(nc, keys_plane, keys_scales)
+        idx2 = lists.tile([P, I // PER_COL], U16, name="idx2")
+        idx = lists.tile([P, I // PER_COL], U16, name="idx")
+        idx3 = lists.tile([P, I // PER_COL], U16, name="idx3")
+        idx4 = lists.tile([P, I // PER_COL], U16, name="idx4")
+        for tile, src in ((idx2, offs2), (idx, offs), (idx3, offs3), (idx4, offs4)):
+            nc.sync.dma_start(tile[:], src)
+
+        q2_codes, q2_scales = quantize_query(nc, sb, raw[:, 1], "q2", Q)
+        q_codes, q_scales = quantize_query(nc, sb, raw[:, 0], "q", 96)
+
+        old_sb = sb.tile([P, Z], F32, name="old_sb", tag="raw_then_old")
+        nc.sync.dma_start(out=old_sb[:], in_=old)
+
+        n_chunks = T // CHUNK
+        banks = [psum.tile([P, CHUNK], F32, name="bank%d" % j) for j in range(n_chunks)]
+        for j in range(n_chunks):
+            cols = slice(j * CHUNK, (j + 1) * CHUNK)
+            nc.tensor.matmul_mx(
+                out=banks[j][:],
+                lhsT=q2_codes[:].bitcast(FP8X4),
+                lhsT_scale=q2_scales[:],
+                rhs=tags[:, 2 * j * CHUNK : 2 * (j + 1) * CHUNK].bitcast(FP4X4),
+                rhs_scale=tags_plane[:, cols],
+                start=True,
+                stop=False,
+            )
+        a = sb.tile([P, T], F32, name="a")
+        tops = sb.tile([P, n_chunks], F32, name="tops")
+        for j in range(n_chunks):
+            cols = slice(j * CHUNK, (j + 1) * CHUNK)
+            nc.tensor.matmul_mx(
+                out=banks[j][:],
+                lhsT=q_codes[:].bitcast(FP8X4),
+                lhsT_scale=q_scales[:],
+                rhs=keys[:, cols].bitcast(FP8X4),
+                rhs_scale=keys_plane[:, cols],
+                start=False,
+                stop=True,
+            )
+            nc.vector.tensor_scalar(
+                out=a[:, cols],
+                in0=banks[j][:],
+                scalar1=1.0,
+                scalar2=None,
+                op0=ALU.mult,
+                op1=ALU.max,
+                accum_out=tops[:, j : j + 1],
+            )
+        neg_ta = sb.tile([P, 1], F32, name="neg_ta")
+        nc.vector.tensor_reduce(out=neg_ta[:], in_=tops[:], axis=mybir.AxisListType.X, op=ALU.max, negate=True)
+
+        for h in range(2):
+            ents = slice(h * HALF // PER_COL, (h + 1) * HALF // PER_COL)
+            e2 = sb.tile([P, HALF], F32, name="e2_%d" % h)
+            e1 = sb.tile([P, HALF], F32, name="e1_%d" % h)
+            neg_e2 = sb.tile([P, HALF], F32, name="neg_e2_%d" % h)
+            nc.scalar.activation(out=e2[:], in_=a[:].indirect(idx2[:, ents]), func=ACT.Exp, bias=neg_ta[:])
+            nc.scalar.activation(out=e1[:], in_=a[:].indirect(idx[:, ents]), func=ACT.Exp, bias=neg_ta[:])
+            if h == 0:
+                nc.vector.tensor_scalar(out=neg_e2[:], in0=e2[:], scalar1=-1.0, scalar2=None, op0=ALU.mult)
+            else:
+                nc.scalar.activation(out=neg_e2[:], in_=e2[:], func=ACT.Copy, scale=-1.0)
+            nc.vector.tensor_tensor(out=f1[:].indirect(idx3[:, ents]), in0=e1[:], in1=neg_e2[:], op=ALU.add)
+
+        cc = sb.tile([P, Z], F32, name="cc")
+        nc.vector.scalar_tensor_tensor(out=cc[:], in0=f1[:], scalar=8.0, in1=old_sb[:], op0=ALU.mult, op1=ALU.add)
+
+        y0 = sb.tile([P, HALF], F32, name="y0")
+        y1 = sb.tile([P, HALF], F32, name="y1")
+        nc.vector.tensor_copy(out=y0[:], in_=cc[:].indirect(idx4[:, 0 : HALF // PER_COL]))
+        nc.scalar.activation(out=y1[:], in_=cc[:].indirect(idx4[:, HALF // PER_COL : I // PER_COL]), func=ACT.Copy)
+        nc.sync.dma_start(out=out[:, 0:HALF], in_=y0[:])
+        nc.scalar.dma_start(out=out[:, HALF:I], in_=y1[:])

@@ -23,11 +23,11 @@ HALF = I // 2
 PER_COL = 16
 
 
-def load_scales(nc, plane, scales):
-    for quad in range(4):
+def load_scales(nc, plane, scales, first):
+    for r in range(4):
         nc.sync.dma_start(
-            out=plane[32 * quad : 32 * quad + 4, :].bitcast(I32),
-            in_=scales[0, 4 * quad : 4 * quad + 4, :].bitcast(I32),
+            out=plane[first + r : P : 32, :].bitcast(I32),
+            in_=scales[0, r:16:4, :].bitcast(I32),
         )
 
 
@@ -74,12 +74,12 @@ def tile_attend_passedover_parts_kernel(
         keys = sb.tile([P, T], U32, name="keys", align_bytes=64)
         nc.sync.dma_start(out=raw[:, 1], in_=query2.rearrange("(p t) q -> p t q", t=PACK))
         nc.sync.dma_start(out=tags[:].bitcast(I32), in_=tags_words[0].bitcast(I32))
-        load_scales(nc, tags_plane, tags_scales)
+        load_scales(nc, tags_plane, tags_scales, 0)
         nc.sync.dma_start(out=raw[:, 0], in_=query.rearrange("(p t) q -> p t q", t=PACK))
         nc.sync.dma_start(
             out=keys[:].bitcast(I32), in_=keys_words[0].rearrange("p n t -> p (n t)").bitcast(I32)
         )
-        load_scales(nc, keys_plane, keys_scales)
+        load_scales(nc, keys_plane, keys_scales, 4)
         idx2 = lists.tile([P, I // PER_COL], U16, name="idx2")
         idx = lists.tile([P, I // PER_COL], U16, name="idx")
         idx3 = lists.tile([P, I // PER_COL], U16, name="idx3")
@@ -115,7 +115,7 @@ def tile_attend_passedover_parts_kernel(
                 lhsT=q_codes[:].bitcast(FP8X4),
                 lhsT_scale=q_scales[:],
                 rhs=keys[:, cols].bitcast(FP8X4),
-                rhs_scale=keys_plane[:, cols],
+                rhs_scale=keys_plane[4:P, cols],
                 start=False,
                 stop=True,
             )

from contextlib import ExitStack

import concourse.mybir as mybir

D, T, Z, I, Q = 512, 1024, 1024, 512, 128
FLOPS = 2 * 2 * D * Q * T

F32 = mybir.dt.float32
BF16 = mybir.dt.bfloat16
I32 = mybir.dt.int32
U32 = mybir.dt.uint32
U16 = mybir.dt.uint16
U8 = mybir.dt.uint8
FP8X4 = mybir.dt.float8_e4m3fn_x4
FP4X4 = mybir.dt.float4_e2m1fn_x4
ALU = mybir.AluOpType
ACT = mybir.ActivationFunctionType

P = 128
PACK = 4
CHUNK = 256
HALF = I // 2
PER_COL = 16


def load_scales(nc, plane, scales, first):
    for r in range(4):
        nc.sync.dma_start(
            out=plane[first + r : P : 32, :].bitcast(I32),
            in_=scales[0, r:16:4, :].bitcast(I32),
        )


def quantize_query(nc, pool, raw, name, split):
    grouped = pool.tile([P, Q, PACK], BF16, name=name + "_grouped", align_bytes=64)
    codes = pool.tile([P, Q], U32, name=name + "_codes", align_bytes=64)
    scales = pool.tile([P, Q], U8, name=name + "_scales", align_bytes=64)
    nc.vector.tensor_copy(
        out=grouped[:, 0:split, :].rearrange("p (c i) t -> p c t i", i=4),
        in_=raw[:, :, 0:split].rearrange("p t (c i) -> p c t i", i=4),
    )
    if split < Q:
        nc.scalar.activation(
            out=grouped[:, split:Q, :].rearrange("p (c i) t -> p c t i", i=4),
            in_=raw[:, :, split:Q].rearrange("p t (c i) -> p c t i", i=4),
            func=ACT.Copy,
        )
    nc.vector.quantize_mx(
        out=codes[:].bitcast(FP8X4),
        scales=scales[:],
        in_=grouped[:].rearrange("p w t -> p (w t)"),
    )
    return codes, scales


def tile_attend_passedover_parts_kernel(
    tc, query, query2, keys_words, keys_scales, tags_words, tags_scales, old, offs, offs2, offs3, offs4, out
):
    nc = tc.nc
    with ExitStack() as ctx:
        lists = ctx.enter_context(tc.tile_pool(name="lists", bufs=1))
        sb = ctx.enter_context(tc.tile_pool(name="sb", bufs=1))
        psum = ctx.enter_context(tc.psum_pool(name="psum", bufs=1))

        tags_plane = sb.tile([P, T], U8, name="tags_plane", align_bytes=64)
        keys_plane = sb.tile([P, T], U8, name="keys_plane", align_bytes=64)
        f1 = sb.tile([P, Z], F32, name="f1")
        nc.vector.memset(tags_plane[:].bitcast(I32), 0)
        nc.vector.memset(keys_plane[:].bitcast(I32), 0)
        nc.vector.memset(f1[:], 0.0)

        raw = sb.tile([P, 2, PACK, Q], F32, name="raw", tag="raw_then_old")
        tags = sb.tile([P, 2 * T], U8, name="tags", align_bytes=64)
        keys = sb.tile([P, T], U32, name="keys", align_bytes=64)
        nc.sync.dma_start(out=raw[:, 1], in_=query2.rearrange("(p t) q -> p t q", t=PACK))
        nc.sync.dma_start(out=tags[:].bitcast(I32), in_=tags_words[0].bitcast(I32))
        load_scales(nc, tags_plane, tags_scales, 0)
        nc.sync.dma_start(out=raw[:, 0], in_=query.rearrange("(p t) q -> p t q", t=PACK))
        nc.sync.dma_start(
            out=keys[:].bitcast(I32), in_=keys_words[0].rearrange("p n t -> p (n t)").bitcast(I32)
        )
        load_scales(nc, keys_plane, keys_scales, 4)
        idx2 = lists.tile([P, I // PER_COL], U16, name="idx2")
        idx = lists.tile([P, I // PER_COL], U16, name="idx")
        idx3 = lists.tile([P, I // PER_COL], U16, name="idx3")
        idx4 = lists.tile([P, I // PER_COL], U16, name="idx4")
        for tile, src in ((idx2, offs2), (idx, offs), (idx3, offs3), (idx4, offs4)):
            nc.sync.dma_start(tile[:], src)

        q2_codes, q2_scales = quantize_query(nc, sb, raw[:, 1], "q2", Q)
        q_codes, q_scales = quantize_query(nc, sb, raw[:, 0], "q", 96)

        old_sb = sb.tile([P, Z], F32, name="old_sb", tag="raw_then_old")
        nc.sync.dma_start(out=old_sb[:], in_=old)

        n_chunks = T // CHUNK
        banks = [psum.tile([P, CHUNK], F32, name="bank%d" % j) for j in range(n_chunks)]
        for j in range(n_chunks):
            cols = slice(j * CHUNK, (j + 1) * CHUNK)
            nc.tensor.matmul_mx(
                out=banks[j][:],
                lhsT=q2_codes[:].bitcast(FP8X4),
                lhsT_scale=q2_scales[:],
                rhs=tags[:, 2 * j * CHUNK : 2 * (j + 1) * CHUNK].bitcast(FP4X4),
                rhs_scale=tags_plane[:, cols],
                start=True,
                stop=False,
            )
        a = sb.tile([P, T], F32, name="a")
        tops = sb.tile([P, n_chunks], F32, name="tops")
        for j in range(n_chunks):
            cols = slice(j * CHUNK, (j + 1) * CHUNK)
            nc.tensor.matmul_mx(
                out=banks[j][:],
                lhsT=q_codes[:].bitcast(FP8X4),
                lhsT_scale=q_scales[:],
                rhs=keys[:, cols].bitcast(FP8X4),
                rhs_scale=keys_plane[4:P, cols],
                start=False,
                stop=True,
            )
            nc.vector.tensor_scalar(
                out=a[:, cols],
                in0=banks[j][:],
                scalar1=1.0,
                scalar2=None,
                op0=ALU.mult,
                op1=ALU.max,
                accum_out=tops[:, j : j + 1],
            )
        neg_ta = sb.tile([P, 1], F32, name="neg_ta")
        nc.vector.tensor_reduce(out=neg_ta[:], in_=tops[:], axis=mybir.AxisListType.X, op=ALU.max, negate=True)

        for h in range(2):
            ents = slice(h * HALF // PER_COL, (h + 1) * HALF // PER_COL)
            e2 = sb.tile([P, HALF], F32, name="e2_%d" % h)
            e1 = sb.tile([P, HALF], F32, name="e1_%d" % h)
            neg_e2 = sb.tile([P, HALF], F32, name="neg_e2_%d" % h)
            nc.scalar.activation(out=e2[:], in_=a[:].indirect(idx2[:, ents]), func=ACT.Exp, bias=neg_ta[:])
            nc.scalar.activation(out=e1[:], in_=a[:].indirect(idx[:, ents]), func=ACT.Exp, bias=neg_ta[:])
            if h == 0:
                nc.vector.tensor_scalar(out=neg_e2[:], in0=e2[:], scalar1=-1.0, scalar2=None, op0=ALU.mult)
            else:
                nc.scalar.activation(out=neg_e2[:], in_=e2[:], func=ACT.Copy, scale=-1.0)
            nc.vector.tensor_tensor(out=f1[:].indirect(idx3[:, ents]), in0=e1[:], in1=neg_e2[:], op=ALU.add)

        cc = sb.tile([P, Z], F32, name="cc")
        nc.vector.scalar_tensor_tensor(out=cc[:], in0=f1[:], scalar=8.0, in1=old_sb[:], op0=ALU.mult, op1=ALU.add)

        y0 = sb.tile([P, HALF], F32, name="y0")
        y1 = sb.tile([P, HALF], F32, name="y1")
        nc.vector.tensor_copy(out=y0[:], in_=cc[:].indirect(idx4[:, 0 : HALF // PER_COL]))
        nc.scalar.activation(out=y1[:], in_=cc[:].indirect(idx4[:, HALF // PER_COL : I // PER_COL]), func=ACT.Copy)
        nc.sync.dma_start(out=out[:, 0:HALF], in_=y0[:])
        nc.scalar.dma_start(out=out[:, HALF:I], in_=y1[:])
